import numpy as np
import ml_dtypes


def mxq(x, axis, fmt="e4m3"):
    dtype, down = {"e4m3": (ml_dtypes.float8_e4m3fn, 7), "e5m2": (ml_dtypes.float8_e5m2, 14)}[fmt]
    v = np.moveaxis(np.asarray(x, np.float32).astype(ml_dtypes.bfloat16).astype(np.float64), axis, -1)
    blocks = v.reshape(v.shape[:-1] + (-1, 32))
    amax = np.abs(blocks).max(-1, keepdims=True)
    byte = np.maximum(np.where(amax > 0, np.frexp(amax)[1] - 1 + 127, 0) - down, 1)
    scale = np.exp2(byte - 127.0)
    codes = (blocks / scale).astype(np.float32).astype(dtype).astype(np.float64)
    return np.moveaxis((codes * scale).reshape(v.shape), -1, axis)


WIDE = False


def mx_kscale(k):
    if not WIDE:
        return np.ones(k)
    levels = np.array([10, -10, 5, -5, 0])
    if k % 512:
        return np.exp2(np.random.permutation(np.resize(levels, k // 32))).repeat(32)
    a = np.empty((k // 512, 16))
    for p in range(k // 512):
        a[p, :8] = np.random.permutation(np.resize(levels, 8))
        for g in range(8):
            far = levels[np.abs(levels - a[p, g]) >= 10]
            a[p, g + 8] = far[np.random.randint(len(far))]
    return np.exp2(a.ravel()).repeat(32)


def f64(x):
    return np.asarray(x).astype(np.float64)


def striped(idx):
    return np.tile(idx.reshape(-1, 16).T, (8, 1)).astype(np.uint16)


def unstriped(offs):
    return offs[:16].T.reshape(-1).astype(np.int64)


def striped8(idx):
    return np.concatenate([x.reshape(-1, 16).T for x in idx]).astype(np.uint16)


def runs(offs, k):
    lists = np.stack([offs[16 * r : 16 * r + 16].T.reshape(-1) for r in range(8)]).astype(np.int64)
    return lists[np.arange(k) % 512 // 64]


def pack_weight(w):
    k, n = w.shape
    w = f64(np.asarray(w, np.float32).astype(ml_dtypes.bfloat16)).reshape(k // 32, 32, n)
    amax = np.abs(w).max(1)
    byte = np.clip(np.where(amax > 0, np.frexp(amax)[1] - 1 + 127 - 7, 1), 1, 254)
    scaled = (w * np.exp2(127.0 - byte)[:, None, :]).reshape(k, n).astype(np.float32)
    words = np.ascontiguousarray(scaled.reshape(k // 512, 128, 4, n).transpose(0, 1, 3, 2)).astype(ml_dtypes.float8_e4m3fn).view(np.uint8)
    return words, np.ascontiguousarray(byte.astype(np.uint8).reshape(k // 512, 16, n))


def unpack_weight(words, scales):
    g, p, n, _ = words.shape
    vals = np.ascontiguousarray(words).view(ml_dtypes.float8_e4m3fn).astype(np.float64) * np.repeat(np.exp2(scales.astype(np.float64) - 127.0), 8, axis=1)[..., None]
    return vals.transpose(0, 1, 3, 2).reshape(g * 512, n)

def planes(y):
    n, m = y.shape
    v = y.astype(np.float32).astype(ml_dtypes.bfloat16).astype(np.float64).reshape(n // 32, 32, m)
    top = np.abs(v).max(1)
    byte = np.clip(np.where(top > 0, np.frexp(top)[1] - 1 + 127 - 7, 1), 1, 254)
    codes = (v * np.exp2(127.0 - byte)[:, None, :]).reshape(n, m).astype(np.float32).astype(ml_dtypes.float8_e4m3fn).view(np.uint8)
    words = codes.reshape(n // 512, 128, 4, m).transpose(0, 1, 3, 2)
    return np.ascontiguousarray(words), np.ascontiguousarray(byte.astype(np.uint8).reshape(n // 512, 16, m))


K, T, S, N, G, H, J = 512, 2048, 256, 512, 2048, 512, 512


def setup_inputs():
    n = np.random.standard_normal
    s = mx_kscale(K)[:, None]
    u = mx_kscale(K)
    packed_xT = pack_weight(n((K, T)) * s)
    packed_dT = pack_weight(n((K, G)) / s)
    packed_w1 = pack_weight(n((H, N)) / np.sqrt(2 * H) / u[:, None])
    packed_w2 = pack_weight(n((K, N)) / np.sqrt(2 * K) / s)
    return {
        "x_words": packed_xT[0],
        "x_scales": packed_xT[1],
        "d_words": packed_dT[0],
        "d_scales": packed_dT[1],
        "gn": (np.random.uniform(0.5, 1.5, (H, 1)) * u[:, None]).astype(np.float32),
        "w1_words": packed_w1[0],
        "w1_scales": packed_w1[1],
        "w2_words": packed_w2[0],
        "w2_scales": packed_w2[1],
        "offs": striped(np.random.permutation(T)[:S]),
        "k1": striped8(np.random.randint(0, G, (8, H))),
        "n1": striped(np.random.permutation(S)),
        "n2": striped(np.random.permutation(S)),
        "two": striped(np.random.permutation(T)[:S]),
        "n3": striped(np.random.randint(0, S, J)),
        "n4": striped(np.random.permutation(S)),
    }


def reference(x_words, x_scales, d_words, d_scales, gn, w1_words, w1_scales, w2_words, w2_scales, offs, k1, n1, n2, two, n3, n4):
    d_k1 = unpack_weight(d_words, d_scales)[np.arange(K)[:, None], runs(k1, K)]
    xq = unpack_weight(x_words, x_scales)[:, unstriped(offs)]
    s = 0.0625 * (d_k1.T @ xq)
    z = f64(gn) * (s - (np.minimum(s[:, unstriped(n1)], s[:, unstriped(n2)])))
    x_two = unpack_weight(x_words, x_scales)[:, unstriped(two)]
    h = unpack_weight(w1_words, w1_scales).T @ mxq(z, 0, "e4m3") + unpack_weight(w2_words, w2_scales).T @ x_two
    mb = h[:, unstriped(n3)]
    mx = mb.reshape(N, S, 2).max(axis=2)
    st = h - mx
    out_0 = np.maximum(st, st[:, unstriped(n4)])
    return (out_0,) + planes(out_0)

@@ -1,0 +1,206 @@
+from contextlib import ExitStack
+
+import concourse.mybir as mybir
+
+K, T, S, N, G, H, J = 512, 2048, 256, 512, 2048, 512, 512
+FLOPS = 2 * 512 * 512 * 256 * 3
+
+F32 = mybir.dt.float32
+BF16 = mybir.dt.bfloat16
+I32 = mybir.dt.int32
+U32 = mybir.dt.uint32
+U16 = mybir.dt.uint16
+U8 = mybir.dt.uint8
+FP8X4 = mybir.dt.float8_e4m3fn_x4
+ALU = mybir.AluOpType
+COPY = mybir.ActivationFunctionType.Copy
+
+P = 128
+HALF = S // 2
+WIDE = J + 16
+
+
+def as_words(words):
+    return words[0].rearrange("p n t -> p (n t)").bitcast(I32)
+
+
+def deal(engine_copy, out, in_):
+    engine_copy(out=out.rearrange("p (t m) -> p m t", t=4), in_=in_.rearrange("p (m t) -> p m t", t=4))
+
+
+def interleave(nc, out, in_):
+    nc.vector.tensor_copy(
+        out=out.rearrange("p (c i t) -> p c t i", i=4, t=4),
+        in_=in_.rearrange("p t (c i) -> p c t i", i=4),
+    )
+
+
+def tile_picked_kmixunderghopm_none_po_kernel(
+    tc, x_words, x_scales, d_words, d_scales, gn, w1_words, w1_scales, w2_words, w2_scales,
+    offs, k1, n1, n2, two, n3, n4, out_0, out_1, out_2,
+):
+    nc = tc.nc
+    with ExitStack() as ctx:
+        held = ctx.enter_context(tc.tile_pool(name="held", bufs=1))
+        psum = ctx.enter_context(tc.psum_pool(name="psum", bufs=1))
+
+        def load_list(src, name):
+            t = held.tile([P, src.shape[1]], U16, name=name)
+            nc.sync.dma_start(t[:], src)
+            return t
+
+        k1_l = load_list(k1, "k1_l")
+        ds_win = held.tile([P, G], U8, name="ds_win")
+        nc.sync.dma_start(ds_win[:].bitcast(I32), d_scales[0].bitcast(I32).unsqueeze(1).broadcast_to([16, 8, G // 4]))
+        offs_l = load_list(offs, "offs_l")
+        two_l = load_list(two, "two_l")
+        n1_l = load_list(n1, "n1_l")
+        n2_l = load_list(n2, "n2_l")
+        xs_win = held.tile([P, T], U8, name="xs_win")
+        nc.vector.memset(xs_win[:].bitcast(I32), 0)
+        nc.sync.dma_start(xs_win[0:P:8, :].bitcast(I32), x_scales[0].bitcast(I32))
+        d_win = held.tile([P, G], I32, name="d_win")
+        nc.sync.dma_start(d_win[:], as_words(d_words))
+        n3_l = load_list(n3, "n3_l")
+        x_win = held.tile([P, T], I32, name="x_win")
+        nc.sync.dma_start(x_win[:], as_words(x_words))
+        w2_raw = held.tile([P, N], I32, name="w2_raw")
+        nc.sync.dma_start(w2_raw[:], as_words(w2_words))
+        n4_l = load_list(n4, "n4_l")
+        gain = held.tile([P, 4], F32, name="gain")
+        nc.gpsimd.dma_start(gain[:], gn.rearrange("(p t) o -> p (t o)", t=4))
+
+        placed = held.tile([P, H + 2 * S], U8, name="placed", align_bytes=64)
+        nc.vector.memset(placed[:].bitcast(I32), 0)
+        h = [held.tile([P, WIDE], F32, name=f"h{t}") for t in range(4)]
+        for t in range(4):
+            nc.vector.memset(h[t][:, S:WIDE], 0.0)
+
+        neg_gain = held.tile([P, 4], F32, name="neg_gain")
+        nc.scalar.activation(out=neg_gain[:], in_=gain[:], func=COPY, scale=-1.0)
+
+        ds_picked = held.tile([P, H], U8, name="ds_picked", tag="reuse_a")
+        nc.vector.tensor_copy(out=ds_picked[:], in_=ds_win[:].indirect(k1_l[:]))
+        xs_picked = held.tile([P, 2 * S], U8, name="xs_picked", tag="reuse_b")
+        nc.vector.tensor_copy(out=xs_picked[:, 0:S], in_=xs_win[:].indirect(offs_l[:]))
+        nc.vector.tensor_copy(out=xs_picked[:, S : 2 * S], in_=xs_win[:].indirect(two_l[:]))
+        staged = held.tile([P, H + 2 * S], U8, name="staged")
+        deal(nc.vector.tensor_copy, staged[:, 0:H], ds_picked[:])
+        nc.vector.tensor_copy(out=staged[:, H : H + 2 * S].bitcast(I32), in_=xs_picked[:].bitcast(I32))
+        for q in range(4):
+            nc.scalar.dma_start(placed[32 * q : 32 * q + 4, :].bitcast(I32), staged[32 * q : 32 * q + 32 : 8, :].bitcast(I32))
+
+        w1_raw = held.tile([P, N], I32, name="w1_raw", tag="reuse_b")
+        nc.sync.dma_start(w1_raw[:], as_words(w1_words))
+        ws_raw = held.tile([P, N], U8, name="ws_raw", tag="reuse_a")
+        nc.gpsimd.memset(ws_raw[:].bitcast(I32), 0)
+        for q in range(4):
+            nc.sync.dma_start(ws_raw[32 * q : 32 * q + 4, :].bitcast(I32), w1_scales[0, 4 * q : 4 * q + 4, :].bitcast(I32))
+            nc.sync.dma_start(ws_raw[32 * q + 4 : 32 * q + 8, :].bitcast(I32), w2_scales[0, 4 * q : 4 * q + 4, :].bitcast(I32))
+
+        d_picked = held.tile([P, H], U32, name="d_picked")
+        nc.vector.tensor_copy(out=d_picked[:], in_=d_win[:].bitcast(U32).indirect(k1_l[:]))
+        d_dealt = held.tile([P, H], U32, name="d_dealt", align_bytes=64)
+        deal(nc.vector.tensor_copy, d_dealt[:], d_picked[:])
+        xq = held.tile([P, S], U32, name="xq", align_bytes=64)
+        nc.vector.tensor_copy(out=xq[:], in_=x_win[:].bitcast(U32).indirect(offs_l[:]))
+
+        s_ps = [psum.tile([P, S], F32, name=f"s_ps{t}", tag=f"bank{t}") for t in range(4)]
+        for t in range(4):
+            cols = slice(P * t, P * (t + 1))
+            nc.tensor.matmul_mx(
+                out=s_ps[t][:], lhsT=d_dealt[:, cols].bitcast(FP8X4), lhsT_scale=placed[:, cols],
+                rhs=xq[:].bitcast(FP8X4), rhs_scale=placed[:, H : H + S], start=True, stop=True,
+            )
+
+        x_two = held.tile([P, S], U32, name="x_two", align_bytes=64)
+        nc.vector.tensor_copy(out=x_two[:], in_=x_win[:].bitcast(U32).indirect(two_l[:]))
+
+        w2_dealt = held.tile([P, N], U32, name="w2_dealt", align_bytes=64)
+        deal(nc.scalar.copy, w2_dealt[:], w2_raw[:].bitcast(U32))
+        w1_dealt = held.tile([P, N], U32, name="w1_dealt", align_bytes=64)
+        deal(nc.gpsimd.tensor_copy, w1_dealt[:], w1_raw[:].bitcast(U32))
+        ws_dealt = held.tile([P, N], U8, name="ws_dealt", align_bytes=64)
+        deal(nc.gpsimd.tensor_copy, ws_dealt[:], ws_raw[:])
+
+        s = held.tile([P, 4, S], F32, name="s")
+        gs = held.tile([P, 4, S], F32, name="gs")
+        z_words = held.tile([P, S], U32, name="z_words", align_bytes=64)
+        z_scales = held.tile([P, S], U8, name="z_scales", align_bytes=64)
+        h_ps = {}
+        for half in range(2):
+            cols = slice(HALF * half, HALF * (half + 1))
+            lc = slice(8 * half, 8 * (half + 1))
+            a = held.tile([P, 4, HALF], F32, name=f"a{half}")
+            b = held.tile([P, 4, HALF], F32, name=f"b{half}")
+            m = held.tile([P, 4, HALF], F32, name=f"m{half}")
+            z = held.tile([P, 4, HALF], BF16, name=f"z{half}")
+            for t in range(4):
+                if half == 0:
+                    nc.scalar.activation(out=s[:, t, :], in_=s_ps[t][:], func=COPY, scale=0.0625)
+                    nc.vector.tensor_scalar(out=gs[:, t, :], in0=s[:, t, :], scalar1=gain[:, t : t + 1], scalar2=None, op0=ALU.mult)
+                nc.scalar.activation(out=a[:, t, :], in_=s[:, t, :].indirect(n1_l[:, lc]), func=COPY)
+                nc.scalar.activation(out=b[:, t, :], in_=s[:, t, :].indirect(n2_l[:, lc]), func=COPY)
+                if half == 1:
+                    nc.vector.tensor_tensor(out=m[:, t, :], in0=a[:, t, :], in1=b[:, t, :], op=ALU.min)
+                    nc.vector.scalar_tensor_tensor(
+                        out=z[:, t, :], in0=m[:, t, :], scalar=neg_gain[:, t : t + 1], in1=gs[:, t, cols], op0=ALU.mult, op1=ALU.add
+                    )
+            if half == 0:
+                nc.vector.tensor_tensor(out=m[:], in0=a[:], in1=b[:], op=ALU.min)
+                for t in range(4):
+                    nc.vector.scalar_tensor_tensor(
+                        out=z[:, t, :], in0=m[:, t, :], scalar=neg_gain[:, t : t + 1], in1=gs[:, t, cols], op0=ALU.mult, op1=ALU.add
+                    )
+            z4 = held.tile([P, 4 * HALF], BF16, name=f"z4{half}", align_bytes=64)
+            interleave(nc, z4[:], z[:])
+            nc.vector.quantize_mx(out=z_words[:, cols].bitcast(FP8X4), scales=z_scales[:, cols], in_=z4[:])
+            for t in range(4):
+                rows = slice(P * t, P * (t + 1))
+                acc = psum.tile([P, HALF], F32, name=f"h_ps{half}{t}", tag=f"bank{4 * (1 - half) + t}")
+                h_ps[half, t] = acc
+                nc.tensor.matmul_mx(
+                    out=acc[:], lhsT=w2_dealt[:, rows].bitcast(FP8X4), lhsT_scale=ws_dealt[4:P, rows],
+                    rhs=x_two[:, cols].bitcast(FP8X4), rhs_scale=placed[:, H + S + HALF * half : H + S + HALF * (half + 1)],
+                    start=True, stop=False,
+                )
+            for t in range(4):
+                rows = slice(P * t, P * (t + 1))
+                nc.tensor.matmul_mx(
+                    out=h_ps[half, t][:], lhsT=w1_dealt[:, rows].bitcast(FP8X4), lhsT_scale=ws_dealt[:, rows],
+                    rhs=z_words[:, cols].bitcast(FP8X4), rhs_scale=z_scales[:, cols], start=False, stop=True,
+                )
+
+        for t in range(4):
+            nc.scalar.activation(out=h[t][:, 0:HALF], in_=h_ps[0, t][:], func=COPY)
+        nc.scalar.activation(out=h[0][:, HALF:S], in_=h_ps[1, 0][:], func=COPY)
+        for t in range(1, 4):
+            nc.vector.tensor_copy(out=h[t][:, HALF:S], in_=h_ps[1, t][:])
+
+        st = held.tile([P, 4, S], F32, name="st")
+        for t in range(4):
+            mb = held.tile([P, J], F32, name=f"mb{t}")
+            nc.scalar.activation(out=mb[:], in_=h[t][:].indirect(n3_l[:]), func=COPY)
+            mx = held.tile([P, S], F32, name=f"mx{t}")
+            nc.vector.tensor_tensor(out=mx[:], in0=mb[:, 0:J:2], in1=mb[:, 1:J:2], op=ALU.max)
+            nc.vector.tensor_tensor(out=st[:, t, :], in0=h[t][:, 0:S], in1=mx[:], op=ALU.subtract)
+
+        y_words = held.tile([P, S], U32, name="y_words", align_bytes=64)
+        y_scales = held.tile([P, S], U8, name="y_scales", align_bytes=64)
+        out_rows = out_0.rearrange("(p t) j -> p t j", t=4)
+        for half in range(2):
+            cols = slice(HALF * half, HALF * (half + 1))
+            lc = slice(8 * half, 8 * (half + 1))
+            far = held.tile([P, 4, HALF], F32, name=f"far{half}")
+            y = held.tile([P, 4, HALF], F32, name=f"y{half}")
+            for t in range(4):
+                nc.scalar.activation(out=far[:, t, :], in_=st[:, t, :].indirect(n4_l[:, lc]), func=COPY)
+            nc.vector.tensor_tensor(out=y[:], in0=st[:, :, cols], in1=far[:], op=ALU.max)
+            nc.sync.dma_start(out_rows[:, :, cols], y[:])
+            y4 = held.tile([P, 4 * HALF], BF16, name=f"y4{half}", align_bytes=64)
+            interleave(nc, y4[:], y[:])
+            nc.vector.quantize_mx(out=y_words[:, cols].bitcast(FP8X4), scales=y_scales[:, cols], in_=y4[:])
+        nc.scalar.dma_start(as_words(out_1), y_words[:].bitcast(I32))
+        for q in range(4):
+            queue = nc.sync if q % 2 == 0 else nc.scalar
+            queue.dma_start(out_2[0, 4 * q : 4 * q + 4, :].bitcast(I32), y_scales[32 * q : 32 * q + 4, :].bitcast(I32))

@@ -18,10 +18,17 @@ COPY = mybir.ActivationFunctionType.Copy
 P = 128
 HALF = S // 2
 WIDE = J + 16
+W_AT = H + 2 * S
+STAGED = W_AT + 2 * N
 
 
 def as_words(words):
     return words[0].rearrange("p n t -> p (n t)").bitcast(I32)
+
+
+def eightfold(scales):
+    rows = scales[0].bitcast(I32)
+    return rows.unsqueeze(1).broadcast_to([16, 8, rows.shape[1]])
 
 
 def deal(engine_copy, out, in_):
@@ -49,54 +56,57 @@ def tile_picked_kmixunderghopm_none_po_kernel(
             nc.sync.dma_start(t[:], src)
             return t
 
-        k1_l = load_list(k1, "k1_l")
-        ds_win = held.tile([P, G], U8, name="ds_win")
-        nc.sync.dma_start(ds_win[:].bitcast(I32), d_scales[0].bitcast(I32).unsqueeze(1).broadcast_to([16, 8, G // 4]))
-        offs_l = load_list(offs, "offs_l")
-        two_l = load_list(two, "two_l")
-        n1_l = load_list(n1, "n1_l")
-        n2_l = load_list(n2, "n2_l")
         xs_win = held.tile([P, T], U8, name="xs_win")
         nc.vector.memset(xs_win[:].bitcast(I32), 0)
+
+        k1_l = load_list(k1, "k1_l")
+        ds_win = held.tile([P, G], U8, name="ds_win")
+        nc.sync.dma_start(ds_win[:].bitcast(I32), eightfold(d_scales))
+        offs_l = load_list(offs, "offs_l")
+        two_l = load_list(two, "two_l")
+        ws_raw = held.tile([P, 2 * N], U8, name="ws_raw")
+        nc.sync.dma_start(ws_raw[:, 0:N].bitcast(I32), eightfold(w1_scales))
+        nc.sync.dma_start(ws_raw[:, N : 2 * N].bitcast(I32), eightfold(w2_scales))
+        gain = held.tile([P, 4], F32, name="gain")
+        nc.sync.dma_start(gain[:], gn.rearrange("(p t) o -> p (t o)", t=4))
         nc.sync.dma_start(xs_win[0:P:8, :].bitcast(I32), x_scales[0].bitcast(I32))
         d_win = held.tile([P, G], I32, name="d_win")
         nc.sync.dma_start(d_win[:], as_words(d_words))
+        n1_l = load_list(n1, "n1_l")
+        n2_l = load_list(n2, "n2_l")
         n3_l = load_list(n3, "n3_l")
         x_win = held.tile([P, T], I32, name="x_win")
         nc.sync.dma_start(x_win[:], as_words(x_words))
         w2_raw = held.tile([P, N], I32, name="w2_raw")
         nc.sync.dma_start(w2_raw[:], as_words(w2_words))
         n4_l = load_list(n4, "n4_l")
-        gain = held.tile([P, 4], F32, name="gain")
-        nc.gpsimd.dma_start(gain[:], gn.rearrange("(p t) o -> p (t o)", t=4))
 
-        placed = held.tile([P, H + 2 * S], U8, name="placed", align_bytes=64)
+        placed = held.tile([P, STAGED], U8, name="placed", align_bytes=64)
         nc.vector.memset(placed[:].bitcast(I32), 0)
         h = [held.tile([P, WIDE], F32, name=f"h{t}") for t in range(4)]
         for t in range(4):
             nc.vector.memset(h[t][:, S:WIDE], 0.0)
 
-        neg_gain = held.tile([P, 4], F32, name="neg_gain")
-        nc.scalar.activation(out=neg_gain[:], in_=gain[:], func=COPY, scale=-1.0)
+        gain16 = held.tile([P, 4], F32, name="gain16")
+        nc.scalar.activation(out=gain16[:], in_=gain[:], func=COPY, scale=0.0625)
 
-        ds_picked = held.tile([P, H], U8, name="ds_picked", tag="reuse_a")
+        ds_picked = held.tile([P, H], U8, name="ds_picked")
         nc.vector.tensor_copy(out=ds_picked[:], in_=ds_win[:].indirect(k1_l[:]))
+        staged = held.tile([P, STAGED], U8, name="staged")
+        deal(nc.vector.tensor_copy, staged[:, 0:H], ds_picked[:])
+        nc.vector.tensor_copy(
+            out=staged[:, W_AT:STAGED].rearrange("p (w t m) -> p w m t", w=2, t=4),
+            in_=ws_raw[:].rearrange("p (w m t) -> p w m t", w=2, t=4),
+        )
         xs_picked = held.tile([P, 2 * S], U8, name="xs_picked", tag="reuse_b")
         nc.vector.tensor_copy(out=xs_picked[:, 0:S], in_=xs_win[:].indirect(offs_l[:]))
         nc.vector.tensor_copy(out=xs_picked[:, S : 2 * S], in_=xs_win[:].indirect(two_l[:]))
-        staged = held.tile([P, H + 2 * S], U8, name="staged")
-        deal(nc.vector.tensor_copy, staged[:, 0:H], ds_picked[:])
         nc.vector.tensor_copy(out=staged[:, H : H + 2 * S].bitcast(I32), in_=xs_picked[:].bitcast(I32))
         for q in range(4):
             nc.scalar.dma_start(placed[32 * q : 32 * q + 4, :].bitcast(I32), staged[32 * q : 32 * q + 32 : 8, :].bitcast(I32))
 
         w1_raw = held.tile([P, N], I32, name="w1_raw", tag="reuse_b")
         nc.sync.dma_start(w1_raw[:], as_words(w1_words))
-        ws_raw = held.tile([P, N], U8, name="ws_raw", tag="reuse_a")
-        nc.gpsimd.memset(ws_raw[:].bitcast(I32), 0)
-        for q in range(4):
-            nc.sync.dma_start(ws_raw[32 * q : 32 * q + 4, :].bitcast(I32), w1_scales[0, 4 * q : 4 * q + 4, :].bitcast(I32))
-            nc.sync.dma_start(ws_raw[32 * q + 4 : 32 * q + 8, :].bitcast(I32), w2_scales[0, 4 * q : 4 * q + 4, :].bitcast(I32))
 
         d_picked = held.tile([P, H], U32, name="d_picked")
         nc.vector.tensor_copy(out=d_picked[:], in_=d_win[:].bitcast(U32).indirect(k1_l[:]))
@@ -119,14 +129,14 @@ def tile_picked_kmixunderghopm_none_po_kernel(
         w2_dealt = held.tile([P, N], U32, name="w2_dealt", align_bytes=64)
         deal(nc.scalar.copy, w2_dealt[:], w2_raw[:].bitcast(U32))
         w1_dealt = held.tile([P, N], U32, name="w1_dealt", align_bytes=64)
-        deal(nc.gpsimd.tensor_copy, w1_dealt[:], w1_raw[:].bitcast(U32))
-        ws_dealt = held.tile([P, N], U8, name="ws_dealt", align_bytes=64)
-        deal(nc.gpsimd.tensor_copy, ws_dealt[:], ws_raw[:])
 
         s = held.tile([P, 4, S], F32, name="s")
-        gs = held.tile([P, 4, S], F32, name="gs")
         z_words = held.tile([P, S], U32, name="z_words", align_bytes=64)
         z_scales = held.tile([P, S], U8, name="z_scales", align_bytes=64)
+        nc.scalar.activation(out=s[:, 0, :], in_=s_ps[0][:], func=COPY)
+        for t in range(1, 4):
+            nc.vector.tensor_copy(out=s[:, t, :], in_=s_ps[t][:])
+        deal(nc.vector.tensor_copy, w1_dealt[:], w1_raw[:].bitcast(U32))
         h_ps = {}
         for half in range(2):
             cols = slice(HALF * half, HALF * (half + 1))
@@ -134,40 +144,35 @@ def tile_picked_kmixunderghopm_none_po_kernel(
             a = held.tile([P, 4, HALF], F32, name=f"a{half}")
             b = held.tile([P, 4, HALF], F32, name=f"b{half}")
             m = held.tile([P, 4, HALF], F32, name=f"m{half}")
-            z = held.tile([P, 4, HALF], BF16, name=f"z{half}")
+            d = held.tile([P, 4, HALF], F32, name=f"d{half}")
             for t in range(4):
-                if half == 0:
-                    nc.scalar.activation(out=s[:, t, :], in_=s_ps[t][:], func=COPY, scale=0.0625)
-                    nc.vector.tensor_scalar(out=gs[:, t, :], in0=s[:, t, :], scalar1=gain[:, t : t + 1], scalar2=None, op0=ALU.mult)
                 nc.scalar.activation(out=a[:, t, :], in_=s[:, t, :].indirect(n1_l[:, lc]), func=COPY)
                 nc.scalar.activation(out=b[:, t, :], in_=s[:, t, :].indirect(n2_l[:, lc]), func=COPY)
-                if half == 1:
-                    nc.vector.tensor_tensor(out=m[:, t, :], in0=a[:, t, :], in1=b[:, t, :], op=ALU.min)
-                    nc.vector.scalar_tensor_tensor(
-                        out=z[:, t, :], in0=m[:, t, :], scalar=neg_gain[:, t : t + 1], in1=gs[:, t, cols], op0=ALU.mult, op1=ALU.add
-                    )
-            if half == 0:
-                nc.vector.tensor_tensor(out=m[:], in0=a[:], in1=b[:], op=ALU.min)
-                for t in range(4):
-                    nc.vector.scalar_tensor_tensor(
-                        out=z[:, t, :], in0=m[:, t, :], scalar=neg_gain[:, t : t + 1], in1=gs[:, t, cols], op0=ALU.mult, op1=ALU.add
-                    )
+            spans = [(0, 2), (2, 4)] if half == 0 else [(0, 2), (2, 3), (3, 4)]
+            for lo, hi in spans:
+                nc.vector.tensor_tensor(out=m[:, lo:hi, :], in0=a[:, lo:hi, :], in1=b[:, lo:hi, :], op=ALU.min)
+                nc.vector.tensor_tensor(out=d[:, lo:hi, :], in0=s[:, lo:hi, cols], in1=m[:, lo:hi, :], op=ALU.subtract)
             z4 = held.tile([P, 4 * HALF], BF16, name=f"z4{half}", align_bytes=64)
-            interleave(nc, z4[:], z[:])
+            nc.vector.tensor_tensor(
+                out=z4[:].rearrange("p (c i t) -> p c t i", i=4, t=4),
+                in0=d[:].rearrange("p t (c i) -> p c t i", i=4),
+                in1=gain16[:].unsqueeze(1).unsqueeze(3).broadcast_to([P, HALF // 4, 4, 4]),
+                op=ALU.mult,
+            )
             nc.vector.quantize_mx(out=z_words[:, cols].bitcast(FP8X4), scales=z_scales[:, cols], in_=z4[:])
             for t in range(4):
                 rows = slice(P * t, P * (t + 1))
                 acc = psum.tile([P, HALF], F32, name=f"h_ps{half}{t}", tag=f"bank{4 * (1 - half) + t}")
                 h_ps[half, t] = acc
                 nc.tensor.matmul_mx(
-                    out=acc[:], lhsT=w2_dealt[:, rows].bitcast(FP8X4), lhsT_scale=ws_dealt[4:P, rows],
+                    out=acc[:], lhsT=w2_dealt[:, rows].bitcast(FP8X4), lhsT_scale=placed[:, W_AT + N + P * t : W_AT + N + P * (t + 1)],
                     rhs=x_two[:, cols].bitcast(FP8X4), rhs_scale=placed[:, H + S + HALF * half : H + S + HALF * (half + 1)],
                     start=True, stop=False,
                 )
             for t in range(4):
                 rows = slice(P * t, P * (t + 1))
                 nc.tensor.matmul_mx(
-                    out=h_ps[half, t][:], lhsT=w1_dealt[:, rows].bitcast(FP8X4), lhsT_scale=ws_dealt[:, rows],
+                    out=h_ps[half, t][:], lhsT=w1_dealt[:, rows].bitcast(FP8X4), lhsT_scale=placed[:, W_AT + P * t : W_AT + P * (t + 1)],
                     rhs=z_words[:, cols].bitcast(FP8X4), rhs_scale=z_scales[:, cols], start=False, stop=True,
                 )
 
@@ -195,12 +200,12 @@ def tile_picked_kmixunderghopm_none_po_kernel(
             y = held.tile([P, 4, HALF], F32, name=f"y{half}")
             for t in range(4):
                 nc.scalar.activation(out=far[:, t, :], in_=st[:, t, :].indirect(n4_l[:, lc]), func=COPY)
-            nc.vector.tensor_tensor(out=y[:], in0=st[:, :, cols], in1=far[:], op=ALU.max)
+                nc.vector.tensor_tensor(out=y[:, t, :], in0=st[:, t, cols], in1=far[:, t, :], op=ALU.max)
             nc.sync.dma_start(out_rows[:, :, cols], y[:])
             y4 = held.tile([P, 4 * HALF], BF16, name=f"y4{half}", align_bytes=64)
             interleave(nc, y4[:], y[:])
             nc.vector.quantize_mx(out=y_words[:, cols].bitcast(FP8X4), scales=y_scales[:, cols], in_=y4[:])
-        nc.scalar.dma_start(as_words(out_1), y_words[:].bitcast(I32))
+            nc.sync.dma_start(as_words(out_1)[:, cols], y_words[:, cols].bitcast(I32))
         for q in range(4):
-            queue = nc.sync if q % 2 == 0 else nc.scalar
+            queue = nc.sync if q == 3 else nc.scalar
             queue.dma_start(out_2[0, 4 * q : 4 * q + 4, :].bitcast(I32), y_scales[32 * q : 32 * q + 4, :].bitcast(I32))

@@ -84,11 +84,15 @@ def tile_picked_kmixunderghopm_none_po_kernel(
         placed = held.tile([P, STAGED], U8, name="placed", align_bytes=64)
         nc.vector.memset(placed[:].bitcast(I32), 0)
         h = [held.tile([P, WIDE], F32, name=f"h{t}") for t in range(4)]
+        s = [held.tile([P, S + 16], F32, name=f"s{t}") for t in range(4)]
+        st = [held.tile([P, S + 16], F32, name=f"st{t}") for t in range(4)]
         for t in range(4):
-            nc.vector.memset(h[t][:, S:WIDE], 0.0)
+            nc.gpsimd.memset(s[t][:, S : S + 16], 0.0)
+            nc.gpsimd.memset(h[t][:, 2 * S : WIDE], 0.0)
+            nc.gpsimd.memset(st[t][:, S : S + 16], 0.0)
 
-        gain16 = held.tile([P, 4], F32, name="gain16")
-        nc.scalar.activation(out=gain16[:], in_=gain[:], func=COPY, scale=0.0625)
+        neg_gain = held.tile([P, 4], F32, name="neg_gain")
+        nc.scalar.activation(out=neg_gain[:], in_=gain[:], func=COPY, scale=-1.0)
 
         ds_picked = held.tile([P, H], U8, name="ds_picked")
         nc.vector.tensor_copy(out=ds_picked[:], in_=ds_win[:].indirect(k1_l[:]))
@@ -130,82 +134,101 @@ def tile_picked_kmixunderghopm_none_po_kernel(
         deal(nc.scalar.copy, w2_dealt[:], w2_raw[:].bitcast(U32))
         w1_dealt = held.tile([P, N], U32, name="w1_dealt", align_bytes=64)
 
-        s = held.tile([P, 4, S], F32, name="s")
+        h_ps = [psum.tile([P, S], F32, name=f"h_ps{t}", tag=f"bank{4 + t}") for t in range(4)]
+        for t in range(4):
+            nc.tensor.matmul_mx(
+                out=h_ps[t][:], lhsT=w2_dealt[:, P * t : P * (t + 1)].bitcast(FP8X4),
+                lhsT_scale=placed[:, W_AT + N + P * t : W_AT + N + P * (t + 1)],
+                rhs=x_two[:].bitcast(FP8X4), rhs_scale=placed[:, H + S : H + 2 * S], start=True, stop=False,
+            )
+
+        nc.scalar.activation(out=s[0][:, 0:S], in_=s_ps[0][:], func=COPY, scale=0.0625)
+        for t in range(1, 4):
+            nc.vector.tensor_scalar(out=s[t][:, 0:S], in0=s_ps[t][:], scalar1=0.0625, scalar2=None, op0=ALU.mult)
+        gs = [h[t][:, S : 2 * S] for t in range(4)]
+        for t in range(4):
+            nc.vector.tensor_scalar(out=gs[t], in0=s[t][:, 0:S], scalar1=gain[:, t : t + 1], scalar2=None, op0=ALU.mult)
+        deal(nc.vector.tensor_copy, w1_dealt[:], w1_raw[:].bitcast(U32))
+
+        pieces = [(t, 0, S) for t in range(3)] + [(3, 0, HALF), (3, HALF, S)]
+        a = held.tile([P, 4, S], F32, name="a")
+        b = held.tile([P, 4, S], F32, name="b")
+        m = held.tile([P, 4, S], F32, name="m")
+        z = held.tile([P, 4, S], BF16, name="z")
+        z4 = held.tile([P, 4 * S], BF16, name="z4", align_bytes=64)
         z_words = held.tile([P, S], U32, name="z_words", align_bytes=64)
         z_scales = held.tile([P, S], U8, name="z_scales", align_bytes=64)
-        nc.scalar.activation(out=s[:, 0, :], in_=s_ps[0][:], func=COPY)
-        for t in range(1, 4):
-            nc.vector.tensor_copy(out=s[:, t, :], in_=s_ps[t][:])
-        deal(nc.vector.tensor_copy, w1_dealt[:], w1_raw[:].bitcast(U32))
-        h_ps = {}
-        for half in range(2):
-            cols = slice(HALF * half, HALF * (half + 1))
-            lc = slice(8 * half, 8 * (half + 1))
-            a = held.tile([P, 4, HALF], F32, name=f"a{half}")
-            b = held.tile([P, 4, HALF], F32, name=f"b{half}")
-            m = held.tile([P, 4, HALF], F32, name=f"m{half}")
-            d = held.tile([P, 4, HALF], F32, name=f"d{half}")
-            for t in range(4):
-                nc.scalar.activation(out=a[:, t, :], in_=s[:, t, :].indirect(n1_l[:, lc]), func=COPY)
-                nc.scalar.activation(out=b[:, t, :], in_=s[:, t, :].indirect(n2_l[:, lc]), func=COPY)
-            spans = [(0, 2), (2, 4)] if half == 0 else [(0, 2), (2, 3), (3, 4)]
-            for lo, hi in spans:
-                nc.vector.tensor_tensor(out=m[:, lo:hi, :], in0=a[:, lo:hi, :], in1=b[:, lo:hi, :], op=ALU.min)
-                nc.vector.tensor_tensor(out=d[:, lo:hi, :], in0=s[:, lo:hi, cols], in1=m[:, lo:hi, :], op=ALU.subtract)
-            z4 = held.tile([P, 4 * HALF], BF16, name=f"z4{half}", align_bytes=64)
-            nc.vector.tensor_tensor(
-                out=z4[:].rearrange("p (c i t) -> p c t i", i=4, t=4),
-                in0=d[:].rearrange("p t (c i) -> p c t i", i=4),
-                in1=gain16[:].unsqueeze(1).unsqueeze(3).broadcast_to([P, HALF // 4, 4, 4]),
-                op=ALU.mult,
+
+        def fetch(t, lo, hi):
+            nc.scalar.activation(out=a[:, t, lo:hi], in_=s[t][:].indirect(n1_l[:, lo // 16 : hi // 16]), func=COPY)
+            nc.scalar.activation(out=b[:, t, lo:hi], in_=s[t][:].indirect(n2_l[:, lo // 16 : hi // 16]), func=COPY)
+
+        def smaller(t, lo, hi):
+            nc.vector.tensor_tensor(out=m[:, t, lo:hi], in0=a[:, t, lo:hi], in1=b[:, t, lo:hi], op=ALU.min)
+
+        def gained(t, lo, hi):
+            nc.vector.scalar_tensor_tensor(
+                out=z[:, t, lo:hi], in0=m[:, t, lo:hi], scalar=neg_gain[:, t : t + 1], in1=gs[t][:, lo:hi], op0=ALU.mult, op1=ALU.add
             )
-            nc.vector.quantize_mx(out=z_words[:, cols].bitcast(FP8X4), scales=z_scales[:, cols], in_=z4[:])
-            for t in range(4):
-                rows = slice(P * t, P * (t + 1))
-                acc = psum.tile([P, HALF], F32, name=f"h_ps{half}{t}", tag=f"bank{4 * (1 - half) + t}")
-                h_ps[half, t] = acc
-                nc.tensor.matmul_mx(
-                    out=acc[:], lhsT=w2_dealt[:, rows].bitcast(FP8X4), lhsT_scale=placed[:, W_AT + N + P * t : W_AT + N + P * (t + 1)],
-                    rhs=x_two[:, cols].bitcast(FP8X4), rhs_scale=placed[:, H + S + HALF * half : H + S + HALF * (half + 1)],
-                    start=True, stop=False,
-                )
-            for t in range(4):
-                rows = slice(P * t, P * (t + 1))
-                nc.tensor.matmul_mx(
-                    out=h_ps[half, t][:], lhsT=w1_dealt[:, rows].bitcast(FP8X4), lhsT_scale=placed[:, W_AT + P * t : W_AT + P * (t + 1)],
-                    rhs=z_words[:, cols].bitcast(FP8X4), rhs_scale=z_scales[:, cols], start=False, stop=True,
-                )
 
+        def weave_z(lo, hi):
+            interleave(nc, z4[:, 4 * lo : 4 * hi], z[:, :, lo:hi])
+
+        def quantise_z(lo, hi):
+            nc.vector.quantize_mx(out=z_words[:, lo:hi].bitcast(FP8X4), scales=z_scales[:, lo:hi], in_=z4[:, 4 * lo : 4 * hi])
+
+        for piece in pieces[:4]:
+            fetch(*piece)
+            smaller(*piece)
+            gained(*piece)
+        weave_z(0, HALF)
+        fetch(*pieces[4])
+        smaller(*pieces[4])
+        quantise_z(0, HALF)
+        gained(*pieces[4])
+        weave_z(HALF, S)
+        quantise_z(HALF, S)
         for t in range(4):
-            nc.scalar.activation(out=h[t][:, 0:HALF], in_=h_ps[0, t][:], func=COPY)
-        nc.scalar.activation(out=h[0][:, HALF:S], in_=h_ps[1, 0][:], func=COPY)
-        for t in range(1, 4):
-            nc.vector.tensor_copy(out=h[t][:, HALF:S], in_=h_ps[1, t][:])
+            nc.tensor.matmul_mx(
+                out=h_ps[t][:], lhsT=w1_dealt[:, P * t : P * (t + 1)].bitcast(FP8X4),
+                lhsT_scale=placed[:, W_AT + P * t : W_AT + P * (t + 1)],
+                rhs=z_words[:].bitcast(FP8X4), rhs_scale=z_scales[:], start=False, stop=True,
+            )
 
-        st = held.tile([P, 4, S], F32, name="st")
+        nc.scalar.activation(out=h[0][:, 0:S], in_=h_ps[0][:], func=COPY)
+        for t in range(1, 4):
+            nc.vector.tensor_copy(out=h[t][:, 0:S], in_=h_ps[t][:])
+
         for t in range(4):
             mb = held.tile([P, J], F32, name=f"mb{t}")
             nc.scalar.activation(out=mb[:], in_=h[t][:].indirect(n3_l[:]), func=COPY)
             mx = held.tile([P, S], F32, name=f"mx{t}")
             nc.vector.tensor_tensor(out=mx[:], in0=mb[:, 0:J:2], in1=mb[:, 1:J:2], op=ALU.max)
-            nc.vector.tensor_tensor(out=st[:, t, :], in0=h[t][:, 0:S], in1=mx[:], op=ALU.subtract)
+            nc.vector.tensor_tensor(out=st[t][:, 0:S], in0=h[t][:, 0:S], in1=mx[:], op=ALU.subtract)
 
+        far = held.tile([P, 4, S], F32, name="far")
+        y = held.tile([P, 4, S], F32, name="y")
+        y4 = held.tile([P, 4 * S], BF16, name="y4", align_bytes=64)
         y_words = held.tile([P, S], U32, name="y_words", align_bytes=64)
         y_scales = held.tile([P, S], U8, name="y_scales", align_bytes=64)
         out_rows = out_0.rearrange("(p t) j -> p t j", t=4)
-        for half in range(2):
-            cols = slice(HALF * half, HALF * (half + 1))
-            lc = slice(8 * half, 8 * (half + 1))
-            far = held.tile([P, 4, HALF], F32, name=f"far{half}")
-            y = held.tile([P, 4, HALF], F32, name=f"y{half}")
-            for t in range(4):
-                nc.scalar.activation(out=far[:, t, :], in_=st[:, t, :].indirect(n4_l[:, lc]), func=COPY)
-                nc.vector.tensor_tensor(out=y[:, t, :], in0=st[:, t, cols], in1=far[:, t, :], op=ALU.max)
-            nc.sync.dma_start(out_rows[:, :, cols], y[:])
-            y4 = held.tile([P, 4 * HALF], BF16, name=f"y4{half}", align_bytes=64)
-            interleave(nc, y4[:], y[:])
-            nc.vector.quantize_mx(out=y_words[:, cols].bitcast(FP8X4), scales=y_scales[:, cols], in_=y4[:])
-            nc.sync.dma_start(as_words(out_1)[:, cols], y_words[:, cols].bitcast(I32))
+
+        def larger(t, lo, hi):
+            nc.scalar.activation(out=far[:, t, lo:hi], in_=st[t][:].indirect(n4_l[:, lo // 16 : hi // 16]), func=COPY)
+            nc.vector.tensor_tensor(out=y[:, t, lo:hi], in0=st[t][:, lo:hi], in1=far[:, t, lo:hi], op=ALU.max)
+            if hi == S:
+                nc.sync.dma_start(out_rows[:, t, :], y[:, t, :])
+
+        def quantise_y(lo, hi):
+            nc.vector.quantize_mx(out=y_words[:, lo:hi].bitcast(FP8X4), scales=y_scales[:, lo:hi], in_=y4[:, 4 * lo : 4 * hi])
+            nc.sync.dma_start(as_words(out_1)[:, lo:hi], y_words[:, lo:hi].bitcast(I32))
+
+        for piece in pieces:
+            larger(*piece)
+        interleave(nc, y4[:, 0 : 4 * HALF], y[:, :, 0:HALF])
+        interleave(nc, y4[:, 4 * HALF : 4 * S], y[:, :, HALF:S])
+        quantise_y(0, HALF)
+        quantise_y(HALF, S)
         for q in range(4):
             queue = nc.sync if q == 3 else nc.scalar
             queue.dma_start(out_2[0, 4 * q : 4 * q + 4, :].bitcast(I32), y_scales[32 * q : 32 * q + 4, :].bitcast(I32))

@@ -57,37 +57,38 @@ def tile_picked_kmixunderghopm_none_po_kernel(
             return t
 
         xs_win = held.tile([P, T], U8, name="xs_win")
-        nc.vector.memset(xs_win[:].bitcast(I32), 0)
+        nc.vector.memset(xs_win[:, 0 : T // 2].bitcast(I32), 0)
+        nc.gpsimd.memset(xs_win[:, T // 2 : T].bitcast(I32), 0)
 
         k1_l = load_list(k1, "k1_l")
         ds_win = held.tile([P, G], U8, name="ds_win")
         nc.sync.dma_start(ds_win[:].bitcast(I32), eightfold(d_scales))
         offs_l = load_list(offs, "offs_l")
         two_l = load_list(two, "two_l")
-        ws_raw = held.tile([P, 2 * N], U8, name="ws_raw")
-        nc.sync.dma_start(ws_raw[:, 0:N].bitcast(I32), eightfold(w1_scales))
-        nc.sync.dma_start(ws_raw[:, N : 2 * N].bitcast(I32), eightfold(w2_scales))
         gain = held.tile([P, 4], F32, name="gain")
         nc.sync.dma_start(gain[:], gn.rearrange("(p t) o -> p (t o)", t=4))
+        n1_l = load_list(n1, "n1_l")
         nc.sync.dma_start(xs_win[0:P:8, :].bitcast(I32), x_scales[0].bitcast(I32))
         d_win = held.tile([P, G], I32, name="d_win")
         nc.sync.dma_start(d_win[:], as_words(d_words))
-        n1_l = load_list(n1, "n1_l")
         n2_l = load_list(n2, "n2_l")
         n3_l = load_list(n3, "n3_l")
+        n4_l = load_list(n4, "n4_l")
         x_win = held.tile([P, T], I32, name="x_win")
         nc.sync.dma_start(x_win[:], as_words(x_words))
-        w2_raw = held.tile([P, N], I32, name="w2_raw")
+        w2_raw = held.tile([P, N], I32, name="w2_raw", tag="reuse_w2")
         nc.sync.dma_start(w2_raw[:], as_words(w2_words))
-        n4_l = load_list(n4, "n4_l")
+        ws_raw = held.tile([P, 2 * N], U8, name="ws_raw")
+        nc.sync.dma_start(ws_raw[:, 0:N].bitcast(I32), eightfold(w1_scales))
+        nc.sync.dma_start(ws_raw[:, N : 2 * N].bitcast(I32), eightfold(w2_scales))
 
-        placed = held.tile([P, STAGED], U8, name="placed", align_bytes=64)
+        placed = held.tile([P, W_AT], U8, name="placed", align_bytes=64)
         nc.vector.memset(placed[:].bitcast(I32), 0)
+        ws_placed = held.tile([P, 2 * N], U8, name="ws_placed", align_bytes=64)
+        nc.vector.memset(ws_placed[:].bitcast(I32), 0)
         h = [held.tile([P, WIDE], F32, name=f"h{t}") for t in range(4)]
-        s = [held.tile([P, S + 16], F32, name=f"s{t}") for t in range(4)]
         st = [held.tile([P, S + 16], F32, name=f"st{t}") for t in range(4)]
         for t in range(4):
-            nc.gpsimd.memset(s[t][:, S : S + 16], 0.0)
             nc.gpsimd.memset(h[t][:, 2 * S : WIDE], 0.0)
             nc.gpsimd.memset(st[t][:, S : S + 16], 0.0)
 
@@ -96,12 +97,8 @@ def tile_picked_kmixunderghopm_none_po_kernel(
 
         ds_picked = held.tile([P, H], U8, name="ds_picked")
         nc.vector.tensor_copy(out=ds_picked[:], in_=ds_win[:].indirect(k1_l[:]))
-        staged = held.tile([P, STAGED], U8, name="staged")
+        staged = held.tile([P, W_AT], U8, name="staged")
         deal(nc.vector.tensor_copy, staged[:, 0:H], ds_picked[:])
-        nc.vector.tensor_copy(
-            out=staged[:, W_AT:STAGED].rearrange("p (w t m) -> p w m t", w=2, t=4),
-            in_=ws_raw[:].rearrange("p (w m t) -> p w m t", w=2, t=4),
-        )
         xs_picked = held.tile([P, 2 * S], U8, name="xs_picked", tag="reuse_b")
         nc.vector.tensor_copy(out=xs_picked[:, 0:S], in_=xs_win[:].indirect(offs_l[:]))
         nc.vector.tensor_copy(out=xs_picked[:, S : 2 * S], in_=xs_win[:].indirect(two_l[:]))
@@ -119,12 +116,14 @@ def tile_picked_kmixunderghopm_none_po_kernel(
         xq = held.tile([P, S], U32, name="xq", align_bytes=64)
         nc.vector.tensor_copy(out=xq[:], in_=x_win[:].bitcast(U32).indirect(offs_l[:]))
 
-        s_ps = [psum.tile([P, S], F32, name=f"s_ps{t}", tag=f"bank{t}") for t in range(4)]
-        for t in range(4):
+        s_parts = [(0, 0, HALF, 0), (0, HALF, S, 7)] + [(t, 0, S, t) for t in range(1, 4)]
+        s_ps = {}
+        for t, lo, hi, bank in s_parts:
             cols = slice(P * t, P * (t + 1))
+            s_ps[t, lo] = psum.tile([P, hi - lo], F32, name=f"s_ps{t}_{lo}", tag=f"bank{bank}")
             nc.tensor.matmul_mx(
-                out=s_ps[t][:], lhsT=d_dealt[:, cols].bitcast(FP8X4), lhsT_scale=placed[:, cols],
-                rhs=xq[:].bitcast(FP8X4), rhs_scale=placed[:, H : H + S], start=True, stop=True,
+                out=s_ps[t, lo][:], lhsT=d_dealt[:, cols].bitcast(FP8X4), lhsT_scale=placed[:, cols],
+                rhs=xq[:, lo:hi].bitcast(FP8X4), rhs_scale=placed[:, H + lo : H + hi], start=True, stop=True,
             )
 
         x_two = held.tile([P, S], U32, name="x_two", align_bytes=64)
@@ -132,19 +131,33 @@ def tile_picked_kmixunderghopm_none_po_kernel(
 
         w2_dealt = held.tile([P, N], U32, name="w2_dealt", align_bytes=64)
         deal(nc.scalar.copy, w2_dealt[:], w2_raw[:].bitcast(U32))
+        s = [held.tile([P, S + 16], F32, name=f"s{t}", tag="reuse_w2" if t == 0 else f"s{t}") for t in range(4)]
+        for t in range(4):
+            nc.gpsimd.memset(s[t][:, S : S + 16], 0.0)
         w1_dealt = held.tile([P, N], U32, name="w1_dealt", align_bytes=64)
 
-        h_ps = [psum.tile([P, S], F32, name=f"h_ps{t}", tag=f"bank{4 + t}") for t in range(4)]
-        for t in range(4):
-            nc.tensor.matmul_mx(
-                out=h_ps[t][:], lhsT=w2_dealt[:, P * t : P * (t + 1)].bitcast(FP8X4),
-                lhsT_scale=placed[:, W_AT + N + P * t : W_AT + N + P * (t + 1)],
-                rhs=x_two[:].bitcast(FP8X4), rhs_scale=placed[:, H + S : H + 2 * S], start=True, stop=False,
-            )
+        ws_staged = held.tile([P, 2 * N], U8, name="ws_staged")
+        nc.vector.tensor_copy(
+            out=ws_staged[:].rearrange("p (w t m) -> p w m t", w=2, t=4),
+            in_=ws_raw[:].rearrange("p (w m t) -> p w m t", w=2, t=4),
+        )
+        for q in range(4):
+            nc.sync.dma_start(ws_placed[32 * q : 32 * q + 4, :].bitcast(I32), ws_staged[32 * q : 32 * q + 32 : 8, :].bitcast(I32))
+        for t, lo, hi, bank in s_parts:
+            if t <= 1:
+                nc.scalar.activation(out=s[t][:, lo:hi], in_=s_ps[t, lo][:], func=COPY, scale=0.0625)
+            else:
+                nc.vector.tensor_scalar(out=s[t][:, lo:hi], in0=s_ps[t, lo][:], scalar1=0.0625, scalar2=None, op0=ALU.mult)
 
-        nc.scalar.activation(out=s[0][:, 0:S], in_=s_ps[0][:], func=COPY, scale=0.0625)
-        for t in range(1, 4):
-            nc.vector.tensor_scalar(out=s[t][:, 0:S], in0=s_ps[t][:], scalar1=0.0625, scalar2=None, op0=ALU.mult)
+        h_parts = [(0, 0, HALF, 4), (0, HALF, S, 0)] + [(t, 0, S, 4 + t) for t in range(1, 4)]
+        h_ps = {}
+        for t, lo, hi, bank in h_parts:
+            h_ps[t, lo] = psum.tile([P, hi - lo], F32, name=f"h_ps{t}_{lo}", tag=f"bank{bank}")
+            nc.tensor.matmul_mx(
+                out=h_ps[t, lo][:], lhsT=w2_dealt[:, P * t : P * (t + 1)].bitcast(FP8X4),
+                lhsT_scale=ws_placed[:, N + P * t : N + P * (t + 1)],
+                rhs=x_two[:, lo:hi].bitcast(FP8X4), rhs_scale=placed[:, H + S + lo : H + S + hi], start=True, stop=False,
+            )
         gs = [h[t][:, S : 2 * S] for t in range(4)]
         for t in range(4):
             nc.vector.tensor_scalar(out=gs[t], in0=s[t][:, 0:S], scalar1=gain[:, t : t + 1], scalar2=None, op0=ALU.mult)
@@ -188,16 +201,16 @@ def tile_picked_kmixunderghopm_none_po_kernel(
         gained(*pieces[4])
         weave_z(HALF, S)
         quantise_z(HALF, S)
-        for t in range(4):
+        for t, lo, hi, bank in h_parts:
             nc.tensor.matmul_mx(
-                out=h_ps[t][:], lhsT=w1_dealt[:, P * t : P * (t + 1)].bitcast(FP8X4),
-                lhsT_scale=placed[:, W_AT + P * t : W_AT + P * (t + 1)],
-                rhs=z_words[:].bitcast(FP8X4), rhs_scale=z_scales[:], start=False, stop=True,
+                out=h_ps[t, lo][:], lhsT=w1_dealt[:, P * t : P * (t + 1)].bitcast(FP8X4),
+                lhsT_scale=ws_placed[:, P * t : P * (t + 1)],
+                rhs=z_words[:, lo:hi].bitcast(FP8X4), rhs_scale=z_scales[:, lo:hi], start=False, stop=True,
             )
-
-        nc.scalar.activation(out=h[0][:, 0:S], in_=h_ps[0][:], func=COPY)
-        for t in range(1, 4):
-            nc.vector.tensor_copy(out=h[t][:, 0:S], in_=h_ps[t][:])
+            if t == 0:
+                nc.scalar.activation(out=h[t][:, lo:hi], in_=h_ps[t, lo][:], func=COPY)
+            else:
+                nc.vector.tensor_copy(out=h[t][:, lo:hi], in_=h_ps[t, lo][:])
 
         for t in range(4):
             mb = held.tile([P, J], F32, name=f"mb{t}")

@@ -3,7 +3,7 @@ from contextlib import ExitStack
 import concourse.mybir as mybir
 
 K, T, S, N, G, H, J = 512, 2048, 256, 512, 2048, 512, 512
-FLOPS = 2 * 512 * 512 * 256 * 3
+FLOPS = 2 * S * (K * H + H * N + K * N)
 
 F32 = mybir.dt.float32
 BF16 = mybir.dt.bfloat16
@@ -16,14 +16,14 @@ ALU = mybir.AluOpType
 COPY = mybir.ActivationFunctionType.Copy
 
 P = 128
+QUARTERS = 4
 HALF = S // 2
-WIDE = J + 16
-W_AT = H + 2 * S
-STAGED = W_AT + 2 * N
+SPARE = 16
+OFFS_AT, TWO_AT, PICKED = H, H + S, H + 2 * S
 
 
 def as_words(words):
-    return words[0].rearrange("p n t -> p (n t)").bitcast(I32)
+    return words[0].rearrange("p n r -> p (n r)").bitcast(I32)
 
 
 def eightfold(scales):
@@ -31,13 +31,18 @@ def eightfold(scales):
     return rows.unsqueeze(1).broadcast_to([16, 8, rows.shape[1]])
 
 
-def deal(engine_copy, out, in_):
-    engine_copy(out=out.rearrange("p (t m) -> p m t", t=4), in_=in_.rearrange("p (m t) -> p m t", t=4))
+def deal(copy, out, in_):
+    copy(out=out.rearrange("p (t m) -> p m t", t=QUARTERS), in_=in_.rearrange("p (m t) -> p m t", t=QUARTERS))
+
+
+def place_scale_rows(queue, placed, staged):
+    for a in range(4):
+        queue.dma_start(placed[32 * a : 32 * a + 4, :].bitcast(I32), staged[32 * a : 32 * a + 32 : 8, :].bitcast(I32))
 
 
 def interleave(nc, out, in_):
     nc.vector.tensor_copy(
-        out=out.rearrange("p (c i t) -> p c t i", i=4, t=4),
+        out=out.rearrange("p (c i t) -> p c t i", i=4, t=QUARTERS),
         in_=in_.rearrange("p t (c i) -> p c t i", i=4),
     )
 
@@ -52,21 +57,21 @@ def tile_picked_kmixunderghopm_none_po_kernel(
         psum = ctx.enter_context(tc.psum_pool(name="psum", bufs=1))
 
         def load_list(src, name):
-            t = held.tile([P, src.shape[1]], U16, name=name)
-            nc.sync.dma_start(t[:], src)
-            return t
+            tile = held.tile([P, src.shape[1]], U16, name=name)
+            nc.sync.dma_start(tile[:], src)
+            return tile
 
         xs_win = held.tile([P, T], U8, name="xs_win")
         nc.vector.memset(xs_win[:, 0 : T // 2].bitcast(I32), 0)
         nc.gpsimd.memset(xs_win[:, T // 2 : T].bitcast(I32), 0)
 
-        k1_l = load_list(k1, "k1_l")
         ds_win = held.tile([P, G], U8, name="ds_win")
         nc.sync.dma_start(ds_win[:].bitcast(I32), eightfold(d_scales))
+        k1_l = load_list(k1, "k1_l")
         offs_l = load_list(offs, "offs_l")
         two_l = load_list(two, "two_l")
-        gain = held.tile([P, 4], F32, name="gain")
-        nc.sync.dma_start(gain[:], gn.rearrange("(p t) o -> p (t o)", t=4))
+        gain = held.tile([P, QUARTERS], F32, name="gain")
+        nc.sync.dma_start(gain[:], gn.rearrange("(p t) o -> p (t o)", t=QUARTERS))
         n1_l = load_list(n1, "n1_l")
         nc.sync.dma_start(xs_win[0:P:8, :].bitcast(I32), x_scales[0].bitcast(I32))
         d_win = held.tile([P, G], I32, name="d_win")
@@ -76,37 +81,37 @@ def tile_picked_kmixunderghopm_none_po_kernel(
         n4_l = load_list(n4, "n4_l")
         x_win = held.tile([P, T], I32, name="x_win")
         nc.sync.dma_start(x_win[:], as_words(x_words))
-        w2_raw = held.tile([P, N], I32, name="w2_raw", tag="reuse_w2")
+        w2_raw = held.tile([P, N], I32, name="w2_raw", tag="w2_then_s0")
         nc.sync.dma_start(w2_raw[:], as_words(w2_words))
         ws_raw = held.tile([P, 2 * N], U8, name="ws_raw")
         nc.sync.dma_start(ws_raw[:, 0:N].bitcast(I32), eightfold(w1_scales))
         nc.sync.dma_start(ws_raw[:, N : 2 * N].bitcast(I32), eightfold(w2_scales))
 
-        placed = held.tile([P, W_AT], U8, name="placed", align_bytes=64)
+        placed = held.tile([P, PICKED], U8, name="placed", align_bytes=64)
         nc.vector.memset(placed[:].bitcast(I32), 0)
         ws_placed = held.tile([P, 2 * N], U8, name="ws_placed", align_bytes=64)
         nc.vector.memset(ws_placed[:].bitcast(I32), 0)
-        h = [held.tile([P, WIDE], F32, name=f"h{t}") for t in range(4)]
-        st = [held.tile([P, S + 16], F32, name=f"st{t}") for t in range(4)]
-        for t in range(4):
-            nc.gpsimd.memset(h[t][:, 2 * S : WIDE], 0.0)
-            nc.gpsimd.memset(st[t][:, S : S + 16], 0.0)
 
-        neg_gain = held.tile([P, 4], F32, name="neg_gain")
+        h = [held.tile([P, J + SPARE], F32, name=f"h{t}") for t in range(QUARTERS)]
+        st = [held.tile([P, S + SPARE], F32, name=f"st{t}") for t in range(QUARTERS)]
+        for t in range(QUARTERS):
+            nc.gpsimd.memset(h[t][:, J : J + SPARE], 0.0)
+            nc.gpsimd.memset(st[t][:, S : S + SPARE], 0.0)
+
+        neg_gain = held.tile([P, QUARTERS], F32, name="neg_gain")
         nc.scalar.activation(out=neg_gain[:], in_=gain[:], func=COPY, scale=-1.0)
 
         ds_picked = held.tile([P, H], U8, name="ds_picked")
         nc.vector.tensor_copy(out=ds_picked[:], in_=ds_win[:].indirect(k1_l[:]))
-        staged = held.tile([P, W_AT], U8, name="staged")
-        deal(nc.vector.tensor_copy, staged[:, 0:H], ds_picked[:])
-        xs_picked = held.tile([P, 2 * S], U8, name="xs_picked", tag="reuse_b")
+        staged = held.tile([P, PICKED], U8, name="staged")
+        deal(nc.vector.tensor_copy, staged[:, 0:OFFS_AT], ds_picked[:])
+        xs_picked = held.tile([P, 2 * S], U8, name="xs_picked", tag="xs_then_w1")
         nc.vector.tensor_copy(out=xs_picked[:, 0:S], in_=xs_win[:].indirect(offs_l[:]))
         nc.vector.tensor_copy(out=xs_picked[:, S : 2 * S], in_=xs_win[:].indirect(two_l[:]))
-        nc.vector.tensor_copy(out=staged[:, H : H + 2 * S].bitcast(I32), in_=xs_picked[:].bitcast(I32))
-        for q in range(4):
-            nc.scalar.dma_start(placed[32 * q : 32 * q + 4, :].bitcast(I32), staged[32 * q : 32 * q + 32 : 8, :].bitcast(I32))
+        nc.vector.tensor_copy(out=staged[:, OFFS_AT:PICKED].bitcast(I32), in_=xs_picked[:].bitcast(I32))
+        place_scale_rows(nc.scalar, placed, staged)
 
-        w1_raw = held.tile([P, N], I32, name="w1_raw", tag="reuse_b")
+        w1_raw = held.tile([P, N], I32, name="w1_raw", tag="xs_then_w1")
         nc.sync.dma_start(w1_raw[:], as_words(w1_words))
 
         d_picked = held.tile([P, H], U32, name="d_picked")
@@ -116,14 +121,14 @@ def tile_picked_kmixunderghopm_none_po_kernel(
         xq = held.tile([P, S], U32, name="xq", align_bytes=64)
         nc.vector.tensor_copy(out=xq[:], in_=x_win[:].bitcast(U32).indirect(offs_l[:]))
 
-        s_parts = [(0, 0, HALF, 0), (0, HALF, S, 7)] + [(t, 0, S, t) for t in range(1, 4)]
+        s_parts = [(0, 0, HALF, 0), (0, HALF, S, 7)] + [(t, 0, S, t) for t in range(1, QUARTERS)]
         s_ps = {}
         for t, lo, hi, bank in s_parts:
             cols = slice(P * t, P * (t + 1))
             s_ps[t, lo] = psum.tile([P, hi - lo], F32, name=f"s_ps{t}_{lo}", tag=f"bank{bank}")
             nc.tensor.matmul_mx(
                 out=s_ps[t, lo][:], lhsT=d_dealt[:, cols].bitcast(FP8X4), lhsT_scale=placed[:, cols],
-                rhs=xq[:, lo:hi].bitcast(FP8X4), rhs_scale=placed[:, H + lo : H + hi], start=True, stop=True,
+                rhs=xq[:, lo:hi].bitcast(FP8X4), rhs_scale=placed[:, OFFS_AT + lo : OFFS_AT + hi], start=True, stop=True,
             )
 
         x_two = held.tile([P, S], U32, name="x_two", align_bytes=64)
@@ -131,76 +136,86 @@ def tile_picked_kmixunderghopm_none_po_kernel(
 
         w2_dealt = held.tile([P, N], U32, name="w2_dealt", align_bytes=64)
         deal(nc.scalar.copy, w2_dealt[:], w2_raw[:].bitcast(U32))
-        s = [held.tile([P, S + 16], F32, name=f"s{t}", tag="reuse_w2" if t == 0 else f"s{t}") for t in range(4)]
-        for t in range(4):
-            nc.gpsimd.memset(s[t][:, S : S + 16], 0.0)
+        s = [held.tile([P, S + SPARE], F32, name=f"s{t}", tag="w2_then_s0" if t == 0 else f"s{t}") for t in range(QUARTERS)]
+        for t in range(QUARTERS):
+            nc.gpsimd.memset(s[t][:, S : S + SPARE], 0.0)
         w1_dealt = held.tile([P, N], U32, name="w1_dealt", align_bytes=64)
 
         ws_staged = held.tile([P, 2 * N], U8, name="ws_staged")
         nc.vector.tensor_copy(
-            out=ws_staged[:].rearrange("p (w t m) -> p w m t", w=2, t=4),
-            in_=ws_raw[:].rearrange("p (w m t) -> p w m t", w=2, t=4),
+            out=ws_staged[:].rearrange("p (w t m) -> p w m t", w=2, t=QUARTERS),
+            in_=ws_raw[:].rearrange("p (w m t) -> p w m t", w=2, t=QUARTERS),
         )
-        for q in range(4):
-            nc.sync.dma_start(ws_placed[32 * q : 32 * q + 4, :].bitcast(I32), ws_staged[32 * q : 32 * q + 32 : 8, :].bitcast(I32))
+        place_scale_rows(nc.sync, ws_placed, ws_staged)
+
         for t, lo, hi, bank in s_parts:
-            if t <= 1:
+            if t < QUARTERS // 2:
                 nc.scalar.activation(out=s[t][:, lo:hi], in_=s_ps[t, lo][:], func=COPY, scale=0.0625)
             else:
                 nc.vector.tensor_scalar(out=s[t][:, lo:hi], in0=s_ps[t, lo][:], scalar1=0.0625, scalar2=None, op0=ALU.mult)
 
-        h_parts = [(0, 0, HALF, 4), (0, HALF, S, 0)] + [(t, 0, S, 4 + t) for t in range(1, 4)]
+        h_parts = [(0, 0, HALF, 4), (0, HALF, S, 0)] + [(t, 0, S, 4 + t) for t in range(1, QUARTERS)]
         h_ps = {}
         for t, lo, hi, bank in h_parts:
             h_ps[t, lo] = psum.tile([P, hi - lo], F32, name=f"h_ps{t}_{lo}", tag=f"bank{bank}")
             nc.tensor.matmul_mx(
                 out=h_ps[t, lo][:], lhsT=w2_dealt[:, P * t : P * (t + 1)].bitcast(FP8X4),
                 lhsT_scale=ws_placed[:, N + P * t : N + P * (t + 1)],
-                rhs=x_two[:, lo:hi].bitcast(FP8X4), rhs_scale=placed[:, H + S + lo : H + S + hi], start=True, stop=False,
+                rhs=x_two[:, lo:hi].bitcast(FP8X4), rhs_scale=placed[:, TWO_AT + lo : TWO_AT + hi], start=True, stop=False,
             )
-        gs = [h[t][:, S : 2 * S] for t in range(4)]
-        for t in range(4):
-            nc.vector.tensor_scalar(out=gs[t], in0=s[t][:, 0:S], scalar1=gain[:, t : t + 1], scalar2=None, op0=ALU.mult)
+        gained_s = [h[t][:, S:J] for t in range(QUARTERS)]
+        for t in range(QUARTERS):
+            nc.vector.tensor_scalar(out=gained_s[t], in0=s[t][:, 0:S], scalar1=gain[:, t : t + 1], scalar2=None, op0=ALU.mult)
         deal(nc.vector.tensor_copy, w1_dealt[:], w1_raw[:].bitcast(U32))
 
-        pieces = [(t, 0, S) for t in range(3)] + [(3, 0, HALF), (3, HALF, S)]
-        a = held.tile([P, 4, S], F32, name="a")
-        b = held.tile([P, 4, S], F32, name="b")
-        m = held.tile([P, 4, S], F32, name="m")
-        z = held.tile([P, 4, S], BF16, name="z")
-        z4 = held.tile([P, 4 * S], BF16, name="z4", align_bytes=64)
+        last = QUARTERS - 1
+        first_half, second_half = (last, 0, HALF), (last, HALF, S)
+        at_n1 = held.tile([P, QUARTERS, S], F32, name="at_n1")
+        at_n2 = held.tile([P, QUARTERS, S], F32, name="at_n2")
+        least = held.tile([P, QUARTERS, S], F32, name="least")
+        z = held.tile([P, QUARTERS, S], BF16, name="z")
+        z4 = held.tile([P, QUARTERS * S], BF16, name="z4", align_bytes=64)
         z_words = held.tile([P, S], U32, name="z_words", align_bytes=64)
         z_scales = held.tile([P, S], U8, name="z_scales", align_bytes=64)
 
-        def fetch(t, lo, hi):
-            nc.scalar.activation(out=a[:, t, lo:hi], in_=s[t][:].indirect(n1_l[:, lo // 16 : hi // 16]), func=COPY)
-            nc.scalar.activation(out=b[:, t, lo:hi], in_=s[t][:].indirect(n2_l[:, lo // 16 : hi // 16]), func=COPY)
+        def fetch_s(t, lo, hi):
+            nc.scalar.activation(out=at_n1[:, t, lo:hi], in_=s[t][:].indirect(n1_l[:, lo // 16 : hi // 16]), func=COPY)
+            nc.scalar.activation(out=at_n2[:, t, lo:hi], in_=s[t][:].indirect(n2_l[:, lo // 16 : hi // 16]), func=COPY)
 
         def smaller(t, lo, hi):
-            nc.vector.tensor_tensor(out=m[:, t, lo:hi], in0=a[:, t, lo:hi], in1=b[:, t, lo:hi], op=ALU.min)
+            nc.vector.tensor_tensor(out=least[:, t, lo:hi], in0=at_n1[:, t, lo:hi], in1=at_n2[:, t, lo:hi], op=ALU.min)
 
-        def gained(t, lo, hi):
+        def make_z(t, lo, hi):
             nc.vector.scalar_tensor_tensor(
-                out=z[:, t, lo:hi], in0=m[:, t, lo:hi], scalar=neg_gain[:, t : t + 1], in1=gs[t][:, lo:hi], op0=ALU.mult, op1=ALU.add
+                out=z[:, t, lo:hi], in0=least[:, t, lo:hi], scalar=neg_gain[:, t : t + 1], in1=gained_s[t][:, lo:hi],
+                op0=ALU.mult, op1=ALU.add,
             )
 
-        def weave_z(lo, hi):
-            interleave(nc, z4[:, 4 * lo : 4 * hi], z[:, :, lo:hi])
+        def interleave_z(lo, hi):
+            interleave(nc, z4[:, QUARTERS * lo : QUARTERS * hi], z[:, :, lo:hi])
 
         def quantise_z(lo, hi):
-            nc.vector.quantize_mx(out=z_words[:, lo:hi].bitcast(FP8X4), scales=z_scales[:, lo:hi], in_=z4[:, 4 * lo : 4 * hi])
+            nc.vector.quantize_mx(
+                out=z_words[:, lo:hi].bitcast(FP8X4), scales=z_scales[:, lo:hi], in_=z4[:, QUARTERS * lo : QUARTERS * hi]
+            )
 
-        for piece in pieces[:4]:
-            fetch(*piece)
+        fetch_s(0, 0, S)
+        fetch_s(1, 0, S)
+        nc.vector.tensor_tensor(out=least[:, 0:2, :], in0=at_n1[:, 0:2, :], in1=at_n2[:, 0:2, :], op=ALU.min)
+        make_z(0, 0, S)
+        make_z(1, 0, S)
+        for piece in [(2, 0, S), first_half]:
+            fetch_s(*piece)
             smaller(*piece)
-            gained(*piece)
-        weave_z(0, HALF)
-        fetch(*pieces[4])
-        smaller(*pieces[4])
+            make_z(*piece)
+        interleave_z(0, HALF)
+        fetch_s(*second_half)
+        smaller(*second_half)
         quantise_z(0, HALF)
-        gained(*pieces[4])
-        weave_z(HALF, S)
+        make_z(*second_half)
+        interleave_z(HALF, S)
         quantise_z(HALF, S)
+
         for t, lo, hi, bank in h_parts:
             nc.tensor.matmul_mx(
                 out=h_ps[t, lo][:], lhsT=w1_dealt[:, P * t : P * (t + 1)].bitcast(FP8X4),
@@ -212,36 +227,43 @@ def tile_picked_kmixunderghopm_none_po_kernel(
             else:
                 nc.vector.tensor_copy(out=h[t][:, lo:hi], in_=h_ps[t, lo][:])
 
-        for t in range(4):
+        for t in range(QUARTERS):
             mb = held.tile([P, J], F32, name=f"mb{t}")
             nc.scalar.activation(out=mb[:], in_=h[t][:].indirect(n3_l[:]), func=COPY)
             mx = held.tile([P, S], F32, name=f"mx{t}")
             nc.vector.tensor_tensor(out=mx[:], in0=mb[:, 0:J:2], in1=mb[:, 1:J:2], op=ALU.max)
             nc.vector.tensor_tensor(out=st[t][:, 0:S], in0=h[t][:, 0:S], in1=mx[:], op=ALU.subtract)
 
-        far = held.tile([P, 4, S], F32, name="far")
-        y = held.tile([P, 4, S], F32, name="y")
-        y4 = held.tile([P, 4 * S], BF16, name="y4", align_bytes=64)
+        at_n4 = held.tile([P, QUARTERS, S], F32, name="at_n4")
+        y = held.tile([P, QUARTERS, S], F32, name="y")
+        y4 = held.tile([P, QUARTERS * S], BF16, name="y4", align_bytes=64)
         y_words = held.tile([P, S], U32, name="y_words", align_bytes=64)
         y_scales = held.tile([P, S], U8, name="y_scales", align_bytes=64)
-        out_rows = out_0.rearrange("(p t) j -> p t j", t=4)
+        out_rows = out_0.rearrange("(p t) j -> p t j", t=QUARTERS)
 
-        def larger(t, lo, hi):
-            nc.scalar.activation(out=far[:, t, lo:hi], in_=st[t][:].indirect(n4_l[:, lo // 16 : hi // 16]), func=COPY)
-            nc.vector.tensor_tensor(out=y[:, t, lo:hi], in0=st[t][:, lo:hi], in1=far[:, t, lo:hi], op=ALU.max)
+        def make_y(t, lo, hi):
+            nc.scalar.activation(out=at_n4[:, t, lo:hi], in_=st[t][:].indirect(n4_l[:, lo // 16 : hi // 16]), func=COPY)
+            nc.vector.tensor_tensor(out=y[:, t, lo:hi], in0=st[t][:, lo:hi], in1=at_n4[:, t, lo:hi], op=ALU.max)
             if hi == S:
                 nc.sync.dma_start(out_rows[:, t, :], y[:, t, :])
 
+        def interleave_y(lo, hi):
+            interleave(nc, y4[:, QUARTERS * lo : QUARTERS * hi], y[:, :, lo:hi])
+
         def quantise_y(lo, hi):
-            nc.vector.quantize_mx(out=y_words[:, lo:hi].bitcast(FP8X4), scales=y_scales[:, lo:hi], in_=y4[:, 4 * lo : 4 * hi])
+            nc.vector.quantize_mx(
+                out=y_words[:, lo:hi].bitcast(FP8X4), scales=y_scales[:, lo:hi], in_=y4[:, QUARTERS * lo : QUARTERS * hi]
+            )
             nc.sync.dma_start(as_words(out_1)[:, lo:hi], y_words[:, lo:hi].bitcast(I32))
 
-        for piece in pieces:
-            larger(*piece)
-        interleave(nc, y4[:, 0 : 4 * HALF], y[:, :, 0:HALF])
-        interleave(nc, y4[:, 4 * HALF : 4 * S], y[:, :, HALF:S])
+        for t in range(last):
+            make_y(t, 0, S)
+        make_y(*first_half)
+        interleave_y(0, HALF)
+        make_y(*second_half)
         quantise_y(0, HALF)
+        interleave_y(HALF, S)
         quantise_y(HALF, S)
-        for q in range(4):
-            queue = nc.sync if q == 3 else nc.scalar
-            queue.dma_start(out_2[0, 4 * q : 4 * q + 4, :].bitcast(I32), y_scales[32 * q : 32 * q + 4, :].bitcast(I32))
+        for a in range(4):
+            queue = nc.sync if a == 3 else nc.scalar
+            queue.dma_start(out_2[0, 4 * a : 4 * a + 4, :].bitcast(I32), y_scales[32 * a : 32 * a + 4, :].bitcast(I32))

from contextlib import ExitStack

import concourse.mybir as mybir

K, T, S, N, G, H, J = 512, 2048, 256, 512, 2048, 512, 512
FLOPS = 2 * S * (K * H + H * N + K * N)

F32 = mybir.dt.float32
BF16 = mybir.dt.bfloat16
I32 = mybir.dt.int32
U32 = mybir.dt.uint32
U16 = mybir.dt.uint16
U8 = mybir.dt.uint8
FP8X4 = mybir.dt.float8_e4m3fn_x4
ALU = mybir.AluOpType
COPY = mybir.ActivationFunctionType.Copy

P = 128
QUARTERS = 4
HALF = S // 2
SPARE = 16
OFFS_AT, TWO_AT, PICKED = H, H + S, H + 2 * S


def as_words(words):
    return words[0].rearrange("p n r -> p (n r)").bitcast(I32)


def eightfold(scales):
    rows = scales[0].bitcast(I32)
    return rows.unsqueeze(1).broadcast_to([16, 8, rows.shape[1]])


def deal(copy, out, in_):
    copy(out=out.rearrange("p (t m) -> p m t", t=QUARTERS), in_=in_.rearrange("p (m t) -> p m t", t=QUARTERS))


def place_scale_rows(queue, placed, staged):
    for a in range(4):
        queue.dma_start(placed[32 * a : 32 * a + 4, :].bitcast(I32), staged[32 * a : 32 * a + 32 : 8, :].bitcast(I32))


def interleave(nc, out, in_):
    nc.vector.tensor_copy(
        out=out.rearrange("p (c i t) -> p c t i", i=4, t=QUARTERS),
        in_=in_.rearrange("p t (c i) -> p c t i", i=4),
    )


def tile_picked_kmixunderghopm_none_po_kernel(
    tc, x_words, x_scales, d_words, d_scales, gn, w1_words, w1_scales, w2_words, w2_scales,
    offs, k1, n1, n2, two, n3, n4, out_0, out_1, out_2,
):
    nc = tc.nc
    with ExitStack() as ctx:
        held = ctx.enter_context(tc.tile_pool(name="held", bufs=1))
        psum = ctx.enter_context(tc.psum_pool(name="psum", bufs=1))

        def load_list(src, name):
            tile = held.tile([P, src.shape[1]], U16, name=name)
            nc.sync.dma_start(tile[:], src)
            return tile

        xs_win = held.tile([P, T], U8, name="xs_win")
        nc.vector.memset(xs_win[:, 0 : T // 2].bitcast(I32), 0)
        nc.gpsimd.memset(xs_win[:, T // 2 : T].bitcast(I32), 0)

        ds_win = held.tile([P, G], U8, name="ds_win")
        nc.sync.dma_start(ds_win[:].bitcast(I32), eightfold(d_scales))
        k1_l = load_list(k1, "k1_l")
        offs_l = load_list(offs, "offs_l")
        two_l = load_list(two, "two_l")
        gain = held.tile([P, QUARTERS], F32, name="gain")
        nc.sync.dma_start(gain[:], gn.rearrange("(p t) o -> p (t o)", t=QUARTERS))
        n1_l = load_list(n1, "n1_l")
        nc.sync.dma_start(xs_win[0:P:8, :].bitcast(I32), x_scales[0].bitcast(I32))
        d_win = held.tile([P, G], I32, name="d_win")
        nc.sync.dma_start(d_win[:], as_words(d_words))
        n2_l = load_list(n2, "n2_l")
        n3_l = load_list(n3, "n3_l")
        n4_l = load_list(n4, "n4_l")
        x_win = held.tile([P, T], I32, name="x_win")
        nc.sync.dma_start(x_win[:], as_words(x_words))
        w2_raw = held.tile([P, N], I32, name="w2_raw", tag="w2_then_s0")
        nc.sync.dma_start(w2_raw[:], as_words(w2_words))
        ws_raw = held.tile([P, 2 * N], U8, name="ws_raw")
        nc.sync.dma_start(ws_raw[:, 0:N].bitcast(I32), eightfold(w1_scales))
        nc.sync.dma_start(ws_raw[:, N : 2 * N].bitcast(I32), eightfold(w2_scales))

        placed = held.tile([P, PICKED], U8, name="placed", align_bytes=64)
        nc.vector.memset(placed[:].bitcast(I32), 0)
        ws_placed = held.tile([P, 2 * N], U8, name="ws_placed", align_bytes=64)
        nc.vector.memset(ws_placed[:].bitcast(I32), 0)

        h = [held.tile([P, J + SPARE], F32, name=f"h{t}") for t in range(QUARTERS)]
        st = [held.tile([P, S + SPARE], F32, name=f"st{t}") for t in range(QUARTERS)]
        for t in range(QUARTERS):
            nc.gpsimd.memset(h[t][:, J : J + SPARE], 0.0)
            nc.gpsimd.memset(st[t][:, S : S + SPARE], 0.0)

        neg_gain = held.tile([P, QUARTERS], F32, name="neg_gain")
        nc.scalar.activation(out=neg_gain[:], in_=gain[:], func=COPY, scale=-1.0)

        ds_picked = held.tile([P, H], U8, name="ds_picked")
        nc.vector.tensor_copy(out=ds_picked[:], in_=ds_win[:].indirect(k1_l[:]))
        staged = held.tile([P, PICKED], U8, name="staged")
        deal(nc.vector.tensor_copy, staged[:, 0:OFFS_AT], ds_picked[:])
        xs_picked = held.tile([P, 2 * S], U8, name="xs_picked", tag="xs_then_w1")
        nc.vector.tensor_copy(out=xs_picked[:, 0:S], in_=xs_win[:].indirect(offs_l[:]))
        nc.vector.tensor_copy(out=xs_picked[:, S : 2 * S], in_=xs_win[:].indirect(two_l[:]))
        nc.vector.tensor_copy(out=staged[:, OFFS_AT:PICKED].bitcast(I32), in_=xs_picked[:].bitcast(I32))
        place_scale_rows(nc.scalar, placed, staged)

        w1_raw = held.tile([P, N], I32, name="w1_raw", tag="xs_then_w1")
        nc.sync.dma_start(w1_raw[:], as_words(w1_words))

        d_picked = held.tile([P, H], U32, name="d_picked")
        nc.vector.tensor_copy(out=d_picked[:], in_=d_win[:].bitcast(U32).indirect(k1_l[:]))
        d_dealt = held.tile([P, H], U32, name="d_dealt", align_bytes=64)
        deal(nc.vector.tensor_copy, d_dealt[:], d_picked[:])
        xq = held.tile([P, S], U32, name="xq", align_bytes=64)
        nc.vector.tensor_copy(out=xq[:], in_=x_win[:].bitcast(U32).indirect(offs_l[:]))

        s_parts = [(0, 0, HALF, 0), (0, HALF, S, 7)] + [(t, 0, S, t) for t in range(1, QUARTERS)]
        s_ps = {}
        for t, lo, hi, bank in s_parts:
            cols = slice(P * t, P * (t + 1))
            s_ps[t, lo] = psum.tile([P, hi - lo], F32, name=f"s_ps{t}_{lo}", tag=f"bank{bank}")
            nc.tensor.matmul_mx(
                out=s_ps[t, lo][:], lhsT=d_dealt[:, cols].bitcast(FP8X4), lhsT_scale=placed[:, cols],
                rhs=xq[:, lo:hi].bitcast(FP8X4), rhs_scale=placed[:, OFFS_AT + lo : OFFS_AT + hi], start=True, stop=True,
            )

        x_two = held.tile([P, S], U32, name="x_two", align_bytes=64)
        nc.vector.tensor_copy(out=x_two[:], in_=x_win[:].bitcast(U32).indirect(two_l[:]))

        w2_dealt = held.tile([P, N], U32, name="w2_dealt", align_bytes=64)
        deal(nc.scalar.copy, w2_dealt[:], w2_raw[:].bitcast(U32))
        s = [held.tile([P, S + SPARE], F32, name=f"s{t}", tag="w2_then_s0" if t == 0 else f"s{t}") for t in range(QUARTERS)]
        for t in range(QUARTERS):
            nc.gpsimd.memset(s[t][:, S : S + SPARE], 0.0)
        w1_dealt = held.tile([P, N], U32, name="w1_dealt", align_bytes=64)

        ws_staged = held.tile([P, 2 * N], U8, name="ws_staged")
        nc.vector.tensor_copy(
            out=ws_staged[:].rearrange("p (w t m) -> p w m t", w=2, t=QUARTERS),
            in_=ws_raw[:].rearrange("p (w m t) -> p w m t", w=2, t=QUARTERS),
        )
        place_scale_rows(nc.sync, ws_placed, ws_staged)

        for t, lo, hi, bank in s_parts:
            if t < QUARTERS // 2:
                nc.scalar.activation(out=s[t][:, lo:hi], in_=s_ps[t, lo][:], func=COPY, scale=0.0625)
            else:
                nc.vector.tensor_scalar(out=s[t][:, lo:hi], in0=s_ps[t, lo][:], scalar1=0.0625, scalar2=None, op0=ALU.mult)

        h_parts = [(0, 0, HALF, 4), (0, HALF, S, 0)] + [(t, 0, S, 4 + t) for t in range(1, QUARTERS)]
        h_ps = {}
        for t, lo, hi, bank in h_parts:
            h_ps[t, lo] = psum.tile([P, hi - lo], F32, name=f"h_ps{t}_{lo}", tag=f"bank{bank}")
            nc.tensor.matmul_mx(
                out=h_ps[t, lo][:], lhsT=w2_dealt[:, P * t : P * (t + 1)].bitcast(FP8X4),
                lhsT_scale=ws_placed[:, N + P * t : N + P * (t + 1)],
                rhs=x_two[:, lo:hi].bitcast(FP8X4), rhs_scale=placed[:, TWO_AT + lo : TWO_AT + hi], start=True, stop=False,
            )
        gained_s = [h[t][:, S:J] for t in range(QUARTERS)]
        for t in range(QUARTERS):
            nc.vector.tensor_scalar(out=gained_s[t], in0=s[t][:, 0:S], scalar1=gain[:, t : t + 1], scalar2=None, op0=ALU.mult)
        deal(nc.vector.tensor_copy, w1_dealt[:], w1_raw[:].bitcast(U32))

        last = QUARTERS - 1
        first_half, second_half = (last, 0, HALF), (last, HALF, S)
        at_n1 = held.tile([P, QUARTERS, S], F32, name="at_n1")
        at_n2 = held.tile([P, QUARTERS, S], F32, name="at_n2")
        least = held.tile([P, QUARTERS, S], F32, name="least")
        z = held.tile([P, QUARTERS, S], BF16, name="z")
        z4 = held.tile([P, QUARTERS * S], BF16, name="z4", align_bytes=64)
        z_words = held.tile([P, S], U32, name="z_words", align_bytes=64)
        z_scales = held.tile([P, S], U8, name="z_scales", align_bytes=64)

        def fetch_s(t, lo, hi):
            nc.scalar.activation(out=at_n1[:, t, lo:hi], in_=s[t][:].indirect(n1_l[:, lo // 16 : hi // 16]), func=COPY)
            nc.scalar.activation(out=at_n2[:, t, lo:hi], in_=s[t][:].indirect(n2_l[:, lo // 16 : hi // 16]), func=COPY)

        def smaller(t, lo, hi):
            nc.vector.tensor_tensor(out=least[:, t, lo:hi], in0=at_n1[:, t, lo:hi], in1=at_n2[:, t, lo:hi], op=ALU.min)

        def make_z(t, lo, hi):
            nc.vector.scalar_tensor_tensor(
                out=z[:, t, lo:hi], in0=least[:, t, lo:hi], scalar=neg_gain[:, t : t + 1], in1=gained_s[t][:, lo:hi],
                op0=ALU.mult, op1=ALU.add,
            )

        def interleave_z(lo, hi):
            interleave(nc, z4[:, QUARTERS * lo : QUARTERS * hi], z[:, :, lo:hi])

        def quantise_z(lo, hi):
            nc.vector.quantize_mx(
                out=z_words[:, lo:hi].bitcast(FP8X4), scales=z_scales[:, lo:hi], in_=z4[:, QUARTERS * lo : QUARTERS * hi]
            )

        fetch_s(0, 0, S)
        fetch_s(1, 0, S)
        nc.vector.tensor_tensor(out=least[:, 0:2, :], in0=at_n1[:, 0:2, :], in1=at_n2[:, 0:2, :], op=ALU.min)
        make_z(0, 0, S)
        make_z(1, 0, S)
        for piece in [(2, 0, S), first_half]:
            fetch_s(*piece)
            smaller(*piece)
            make_z(*piece)
        interleave_z(0, HALF)
        fetch_s(*second_half)
        smaller(*second_half)
        quantise_z(0, HALF)
        make_z(*second_half)
        interleave_z(HALF, S)
        quantise_z(HALF, S)

        for t, lo, hi, bank in h_parts:
            nc.tensor.matmul_mx(
                out=h_ps[t, lo][:], lhsT=w1_dealt[:, P * t : P * (t + 1)].bitcast(FP8X4),
                lhsT_scale=ws_placed[:, P * t : P * (t + 1)],
                rhs=z_words[:, lo:hi].bitcast(FP8X4), rhs_scale=z_scales[:, lo:hi], start=False, stop=True,
            )
            if t == 0:
                nc.scalar.activation(out=h[t][:, lo:hi], in_=h_ps[t, lo][:], func=COPY)
            else:
                nc.vector.tensor_copy(out=h[t][:, lo:hi], in_=h_ps[t, lo][:])

        for t in range(QUARTERS):
            mb = held.tile([P, J], F32, name=f"mb{t}")
            nc.scalar.activation(out=mb[:], in_=h[t][:].indirect(n3_l[:]), func=COPY)
            mx = held.tile([P, S], F32, name=f"mx{t}")
            nc.vector.tensor_tensor(out=mx[:], in0=mb[:, 0:J:2], in1=mb[:, 1:J:2], op=ALU.max)
            nc.vector.tensor_tensor(out=st[t][:, 0:S], in0=h[t][:, 0:S], in1=mx[:], op=ALU.subtract)

        at_n4 = held.tile([P, QUARTERS, S], F32, name="at_n4")
        y = held.tile([P, QUARTERS, S], F32, name="y")
        y4 = held.tile([P, QUARTERS * S], BF16, name="y4", align_bytes=64)
        y_words = held.tile([P, S], U32, name="y_words", align_bytes=64)
        y_scales = held.tile([P, S], U8, name="y_scales", align_bytes=64)
        out_rows = out_0.rearrange("(p t) j -> p t j", t=QUARTERS)

        def make_y(t, lo, hi):
            nc.scalar.activation(out=at_n4[:, t, lo:hi], in_=st[t][:].indirect(n4_l[:, lo // 16 : hi // 16]), func=COPY)
            nc.vector.tensor_tensor(out=y[:, t, lo:hi], in0=st[t][:, lo:hi], in1=at_n4[:, t, lo:hi], op=ALU.max)
            if hi == S:
                nc.sync.dma_start(out_rows[:, t, :], y[:, t, :])

        def interleave_y(lo, hi):
            interleave(nc, y4[:, QUARTERS * lo : QUARTERS * hi], y[:, :, lo:hi])

        def quantise_y(lo, hi):
            nc.vector.quantize_mx(
                out=y_words[:, lo:hi].bitcast(FP8X4), scales=y_scales[:, lo:hi], in_=y4[:, QUARTERS * lo : QUARTERS * hi]
            )
            nc.sync.dma_start(as_words(out_1)[:, lo:hi], y_words[:, lo:hi].bitcast(I32))

        for t in range(last):
            make_y(t, 0, S)
        make_y(*first_half)
        interleave_y(0, HALF)
        make_y(*second_half)
        quantise_y(0, HALF)
        interleave_y(HALF, S)
        quantise_y(HALF, S)
        for a in range(4):
            queue = nc.sync if a == 3 else nc.scalar
            queue.dma_start(out_2[0, 4 * a : 4 * a + 4, :].bitcast(I32), y_scales[32 * a : 32 * a + 4, :].bitcast(I32))
